import numpy as np
import ml_dtypes


def mxq(x, axis, fmt="e4m3"):
    dtype, down = {"e4m3": (ml_dtypes.float8_e4m3fn, 7), "e5m2": (ml_dtypes.float8_e5m2, 14)}[fmt]
    v = np.moveaxis(np.asarray(x, np.float32).astype(ml_dtypes.bfloat16).astype(np.float64), axis, -1)
    blocks = v.reshape(v.shape[:-1] + (-1, 32))
    amax = np.abs(blocks).max(-1, keepdims=True)
    byte = np.maximum(np.where(amax > 0, np.frexp(amax)[1] - 1 + 127, 0) - down, 1)
    scale = np.exp2(byte - 127.0)
    codes = (blocks / scale).astype(np.float32).astype(dtype).astype(np.float64)
    return np.moveaxis((codes * scale).reshape(v.shape), -1, axis)


WIDE = False


def mx_kscale(k):
    if not WIDE:
        return np.ones(k)
    levels = np.array([10, -10, 5, -5, 0])
    if k % 512:
        return np.exp2(np.random.permutation(np.resize(levels, k // 32))).repeat(32)
    a = np.empty((k // 512, 16))
    for p in range(k // 512):
        a[p, :8] = np.random.permutation(np.resize(levels, 8))
        for g in range(8):
            far = levels[np.abs(levels - a[p, g]) >= 10]
            a[p, g + 8] = far[np.random.randint(len(far))]
    return np.exp2(a.ravel()).repeat(32)


BF16 = ml_dtypes.bfloat16


def bf(x):
    return np.asarray(x, np.float32).astype(BF16)


def f64(x):
    return np.asarray(x).astype(np.float64)


E2M1 = np.array([0.0, 0.5, 1.0, 1.5, 2.0, 3.0, 4.0, 6.0, -0.0, -0.5, -1.0, -1.5, -2.0, -3.0, -4.0, -6.0])


def pack_weight(w, fmt):
    k, n = w.shape
    w = f64(bf(w)).reshape(k // 32, 32, n)
    amax = np.abs(w).max(1)
    if fmt == "e4m3":
        byte = np.frexp(amax)[1] - 1 + 127 - 7
    else:
        mant, ex = np.frexp(amax / 6.0)
        byte = np.where(mant > 0.5, ex, ex - 1) + 127
    byte = np.clip(np.where(amax > 0, byte, 1), 1, 254)
    scaled = (w * np.exp2(127.0 - byte)[:, None, :]).reshape(k, n).astype(np.float32)
    by_word = np.ascontiguousarray(scaled.reshape(k // 512, 128, 4, n).transpose(0, 1, 3, 2))
    if fmt == "e4m3":
        words = by_word.astype(ml_dtypes.float8_e4m3fn).view(np.uint8)
    else:
        c = by_word.astype(ml_dtypes.float4_e2m1fn).view(np.uint8) & 0xF
        words = c[..., 0::2] | (c[..., 1::2] << 4)
    return np.ascontiguousarray(words), np.ascontiguousarray(byte.astype(np.uint8).reshape(k // 512, 16, n))


def unpack_weight(words, scales, fmt):
    g, p, n, _ = words.shape
    if fmt == "e4m3":
        vals = np.ascontiguousarray(words).view(ml_dtypes.float8_e4m3fn).astype(np.float64)
    else:
        nib = np.empty((g, p, n, 4), np.uint8)
        nib[..., 0::2] = words & 0xF
        nib[..., 1::2] = words >> 4
        vals = E2M1[nib]
    vals = vals * np.repeat(np.exp2(scales.astype(np.float64) - 127.0), 8, axis=1)[..., None]
    return vals.transpose(0, 1, 3, 2).reshape(g * 512, n)
def pack4(w):
    words, scales = pack_weight(w, "e2m1")
    return words.reshape(words.shape[0], 128, -1), scales


def unpack4(words, scales):
    return unpack_weight(words.reshape(words.shape[0], 128, -1, 2), scales, "e2m1")


def planes(Y):
    n, m = Y.shape
    b = f64(bf(Y)).reshape(n // 32, 32, m)
    amax = np.abs(b).max(1)
    byte = np.clip(np.where(amax > 0, np.frexp(amax)[1] - 1 + 127 - 7, 1), 1, 254)
    codes = (b * np.exp2(127.0 - byte)[:, None, :]).reshape(n, m).astype(np.float32).astype(ml_dtypes.float8_e4m3fn).view(np.uint8)
    words = codes.reshape(n // 512, 128, 4, m).transpose(0, 1, 3, 2)
    return np.ascontiguousarray(words), np.ascontiguousarray(byte.astype(np.uint8).reshape(n // 512, 16, m))


K, T, B = 2048, 1024, 1536


def setup_inputs():
    s = mx_kscale(K)
    t = mx_kscale(T)
    l = np.random.randn(K, T) / np.sqrt(K) * s[:, None] * t[None, :]
    o = np.random.randn(K, B) / s[:, None]
    l_words, l_scales = pack4(l)
    o_words, o_scales = pack4(o)
    u = np.random.randn(T, B) * t[:, None]
    qf = np.random.randn(T, T) / np.sqrt(T) / t[:, None]
    c = np.random.randn(T, B)
    gain = np.exp(0.8 * np.random.randn(T))
    return {"l_words": l_words, "l_scales": l_scales, "o_words": o_words, "o_scales": o_scales,
            "u": bf(u), "qf": bf(qf), "c": bf(c), "gain": bf(gain)}

def reference(l_words, l_scales, o_words, o_scales, u, qf, c, gain):
    l = unpack4(l_words, l_scales)
    o = unpack4(o_words, o_scales)
    r = (l.T @ o) - f64(u)
    d = mxq(f64(qf), 0, "e4m3").T @ mxq(r, 0, "e4m3")
    y = f64(gain)[:, None] * (f64(c) - d)
    Y = y
    words, scales = planes(Y)
    return y, words, scales

@@ -1,0 +1,409 @@
+from contextlib import ExitStack
+
+import concourse.mybir as mybir
+
+K, T, B = 2048, 1024, 1536
+FLOPS = 2 * K * T * B + 2 * T * T * B
+
+F32 = mybir.dt.float32
+BF16 = mybir.dt.bfloat16
+I32 = mybir.dt.int32
+U8 = mybir.dt.uint8
+FP8X4 = mybir.dt.float8_e4m3fn_x4
+FP4X4 = mybir.dt.float4_e2m1fn_x4
+ALU = mybir.AluOpType
+ACT = mybir.ActivationFunctionType
+
+P = 128
+PACK = 4
+PASS = P * PACK
+G1 = K // PASS
+H = T // PASS
+BLK = 128
+PAIR = 256
+BANKS = 8
+
+O_CHUNKS = [(0, 256), (256, 512), (512, 1024), (1024, 1536)]
+OS_CHUNKS = [(0, 512), (512, 1536)]
+U_CHUNKS = [(0, 512), (512, 1024), (1024, 1536)]
+C_CHUNKS = [(0, 512), (512, 1024), (1024, 1536)]
+
+
+def find(chunks, col):
+    return [n for n, (a, b) in enumerate(chunks) if a <= col < b][0]
+
+
+def tile_disturbance_observer_command_k5_kernel(
+    tc, l_words, l_scales, o_words, o_scales, u, qf, c, gain, out_0, out_1, out_2
+):
+    nc = tc.nc
+    with ExitStack() as ctx:
+        keep = ctx.enter_context(tc.tile_pool(name="keep", bufs=1))
+        ring = ctx.enter_context(tc.tile_pool(name="ring", bufs=3))
+        psum = ctx.enter_context(tc.psum_pool(name="psum", bufs=1))
+        ctx.enter_context(tc.manual_schedule())
+
+        def kept(name, shape, dtype):
+            return keep.tile(shape, dtype, name=name, align_bytes=64)
+
+        l_raw = [kept("l_raw%d" % h, [P, G1, 2 * PASS], U8) for h in range(H)]
+        ls_raw = [kept("ls_raw%d" % h, [P, G1, PASS], U8) for h in range(H)]
+        l_codes = [kept("l_codes%d" % h, [P, PACK, G1, 2 * P], U8) for h in range(H)]
+        l_plane = [kept("l_plane%d" % h, [P, PACK, G1, P], U8) for h in range(H)]
+        o_codes = [kept("o_codes%d" % n, [P, G1, 2 * (b - a)], U8) for n, (a, b) in enumerate(O_CHUNKS)]
+        o_plane = [kept("o_plane%d" % n, [P, G1, b - a], U8) for n, (a, b) in enumerate(OS_CHUNKS)]
+        u_sb = [[kept("u%d_%d" % (n, h), [P, PACK, b - a], BF16) for h in range(H)] for n, (a, b) in enumerate(U_CHUNKS)]
+        c_sb = [[kept("c%d_%d" % (n, h), [P, PACK, b - a], BF16) for h in range(H)] for n, (a, b) in enumerate(C_CHUNKS)]
+        q_raw = [kept("q_raw%d" % g, [P, PACK, T], BF16) for g in range(H)]
+        q_codes = [[kept("q_codes%d_%d" % (g, h), [P, PASS], I32) for h in range(H)] for g in range(H)]
+        q_plane = [[kept("q_plane%d_%d" % (g, h), [P, PASS], U8) for h in range(H)] for g in range(H)]
+        r_codes = [kept("r_codes%d" % g, [P, B], I32) for g in range(H)]
+        r_plane = [kept("r_plane%d" % g, [P, B], U8) for g in range(H)]
+        y_sb = [kept("y%d" % h, [P, PACK, B], F32) for h in range(H)]
+        y_codes = kept("y_codes", [P, H, B], I32)
+        y_plane = kept("y_plane", [P, H, B], U8)
+        gain_raw = kept("gain_raw", [P, H, PACK], BF16)
+        gain_pos = kept("gain_pos", [P, H, PACK], F32)
+        gain_neg = kept("gain_neg", [P, H, PACK], F32)
+
+        used_banks = []
+        s1_bank = {}
+        s2_bank = {}
+        r_bf = {}
+        y_bf = {}
+        q_bf = {}
+
+        def new_bank():
+            n = len(used_banks) % BANKS
+            used_banks.append(n)
+            return psum.tile([P, PASS], F32, name="bank%d" % n, tag="bank%d" % n)
+
+        def words(ap, pattern):
+            return ap.rearrange(pattern).bitcast(I32)
+
+        def clear(plane):
+            nc.vector.memset(words(plane[:], "p g n -> p (g n)"), 0)
+
+        def load_plane(plane, scales, a, b, q):
+            nc.sync.dma_start(
+                out=plane[32 * q : 32 * q + 4, :, :].bitcast(I32),
+                in_=scales[:, 4 * q : 4 * q + 4, a:b].rearrange("g r n -> r g n").bitcast(I32),
+            )
+
+        def load_codes(dst, src, a, b):
+            nc.sync.dma_start(
+                out=dst[:].bitcast(I32),
+                in_=src[:, :, 2 * a : 2 * b].rearrange("g p n -> p g n").bitcast(I32),
+            )
+
+        def load_r_order(dst, src, g, a, b):
+            rows = src[PASS * g : PASS * (g + 1), a:b].rearrange("(c t e) n -> e c t n", t=PACK, e=4)
+            for e in range(4):
+                nc.sync.dma_start(out=dst[e:P:4, :, :], in_=rows[e])
+
+        def load_c(n, h):
+            a, b = C_CHUNKS[n]
+            nc.sync.dma_start(
+                out=c_sb[n][h][:],
+                in_=c[PASS * h : PASS * (h + 1), a:b].rearrange("(p t) n -> p t n", t=PACK),
+            )
+
+        def load_ls(h, q):
+            load_plane(ls_raw[h], l_scales, PASS * h, PASS * (h + 1), q)
+
+        def load_os(n, q):
+            load_plane(o_plane[n], o_scales, OS_CHUNKS[n][0], OS_CHUNKS[n][1], q)
+
+        def load_l(h):
+            load_codes(l_raw[h], l_words, PASS * h, PASS * (h + 1))
+
+        def load_o(n):
+            load_codes(o_codes[n], o_words, O_CHUNKS[n][0], O_CHUNKS[n][1])
+
+        def load_u(n, h):
+            load_r_order(u_sb[n][h], u, h, U_CHUNKS[n][0], U_CHUNKS[n][1])
+
+        def load_q(g):
+            load_r_order(q_raw[g], qf, g, 0, T)
+
+        def order_l(h, t0, t1):
+            src = words(l_raw[h][:], "p g n -> p (g n)").rearrange("p (x t e) -> p t x e", t=PACK, e=2)
+            dst = words(l_codes[h][:], "p t g n -> p (t g n)").rearrange("p (t x e) -> p t x e", t=PACK, e=2)
+            nc.vector.tensor_copy(out=dst[:, t0:t1], in_=src[:, t0:t1])
+
+        def order_ls(h):
+            src = words(ls_raw[h][:], "p g n -> p (g n)").rearrange("p (x t) -> p t x", t=PACK)
+            dst = words(l_plane[h][:], "p t g n -> p (t g n)").rearrange("p (t x) -> p t x", t=PACK)
+            nc.vector.tensor_copy(out=dst, in_=src)
+
+        def stage1(blk, h):
+            bank = new_bank()
+            s1_bank[blk, h] = bank
+            col = blk * BLK
+            n = find(O_CHUNKS, col)
+            ns = find(OS_CHUNKS, col)
+            oc = col - O_CHUNKS[n][0]
+            sc = col - OS_CHUNKS[ns][0]
+            for t in range(PACK):
+                for g in range(G1):
+                    nc.tensor.matmul_mx(
+                        out=bank[:, BLK * t : BLK * (t + 1)],
+                        lhsT=l_codes[h][:, t, g, :].bitcast(FP4X4),
+                        lhsT_scale=l_plane[h][:, t, g, :],
+                        rhs=o_codes[n][:, g, 2 * oc : 2 * (oc + BLK)].bitcast(FP4X4),
+                        rhs_scale=o_plane[ns][:, g, sc : sc + BLK],
+                        start=(g == 0),
+                        stop=(g == G1 - 1),
+                    )
+
+        def residual(blk, h):
+            if blk % 2 == 0:
+                r_bf[blk // 2, h] = ring.tile([P, PAIR * PACK], BF16, name="r_bf", tag="r_bf", align_bytes=64)
+            col = blk * BLK
+            n = find(U_CHUNKS, col)
+            uc = col - U_CHUNKS[n][0]
+            half = PASS * (blk % 2)
+            nc.vector.tensor_tensor(
+                out=r_bf[blk // 2, h][:, half : half + PASS].rearrange("p (x i t) -> p x t i", i=4, t=PACK),
+                in0=s1_bank[blk, h][:].rearrange("p (t x i) -> p x t i", t=PACK, i=4),
+                in1=u_sb[n][h][:, :, uc : uc + BLK].rearrange("p t (x i) -> p x t i", i=4),
+                op=ALU.subtract,
+            )
+
+        def quantize_r(pair, h, lo=0, hi=PAIR):
+            a = pair * PAIR
+            nc.vector.quantize_mx(
+                out=r_codes[h][:, a + lo : a + hi].bitcast(FP8X4),
+                scales=r_plane[h][:, a + lo : a + hi],
+                in_=r_bf[pair, h][:, PACK * lo : PACK * hi],
+            )
+
+        def group_q(g, h, copy):
+            q_bf[g, h] = ring.tile([P, PASS * PACK], BF16, name="q_bf", tag="q_bf", align_bytes=64)
+            copy(
+                out=q_bf[g, h][:].rearrange("p (t m j) -> p t m j", t=PACK, j=PACK),
+                in_=q_raw[g][:, :, PASS * h : PASS * (h + 1)].rearrange("p j (m t) -> p t m j", t=PACK),
+            )
+
+        def quantize_q(g, h):
+            nc.vector.quantize_mx(out=q_codes[g][h][:].bitcast(FP8X4), scales=q_plane[g][h][:], in_=q_bf[g, h][:])
+
+        def scale_c(h, a, b):
+            n = find(C_CHUNKS, a)
+            c0 = C_CHUNKS[n][0]
+            for t in range(PACK):
+                nc.scalar.activation(
+                    out=y_sb[h][:, t, a:b],
+                    in_=c_sb[n][h][:, t, a - c0 : b - c0],
+                    func=ACT.Copy,
+                    scale=gain_pos[:, h, t : t + 1],
+                )
+
+        def stage2(h, a, b):
+            w = b - a
+            per_bank = PASS // w
+            for t in range(PACK):
+                if t % per_bank == 0:
+                    bank = new_bank()
+                dst = bank[:, w * (t % per_bank) : w * (t % per_bank + 1)]
+                s2_bank[h, a, t] = dst
+                for g in range(H):
+                    nc.tensor.matmul_mx(
+                        out=dst,
+                        lhsT=q_codes[g][h][:, P * t : P * (t + 1)].bitcast(FP8X4),
+                        lhsT_scale=q_plane[g][h][:, P * t : P * (t + 1)],
+                        rhs=r_codes[g][:, a:b].bitcast(FP8X4),
+                        rhs_scale=r_plane[g][:, a:b],
+                        start=(g == 0),
+                        stop=(g == H - 1),
+                    )
+
+        def command(h, a, b, t0=0, t1=PACK):
+            for t in range(t0, t1):
+                nc.vector.scalar_tensor_tensor(
+                    out=y_sb[h][:, t, a:b],
+                    in0=s2_bank[h, a, t],
+                    scalar=gain_neg[:, h, t : t + 1],
+                    in1=y_sb[h][:, t, a:b],
+                    op0=ALU.mult,
+                    op1=ALU.add,
+                )
+
+        def store_y(h, a, b):
+            nc.sync.dma_start(
+                out=out_0[PASS * h : PASS * (h + 1), a:b].rearrange("(p t) n -> p t n", t=PACK),
+                in_=y_sb[h][:, :, a:b],
+            )
+
+        def round_y(h, a, b):
+            y_bf[h, a] = ring.tile([P, (b - a) * PACK], BF16, name="y_bf", tag="y_bf", bufs=4, align_bytes=64)
+            nc.scalar.copy(
+                out=y_bf[h, a][:].rearrange("p (x i t) -> p x t i", i=4, t=PACK),
+                in_=y_sb[h][:, :, a:b].rearrange("p t (x i) -> p x t i", i=4),
+            )
+
+        def quantize_y(h, a, b):
+            nc.vector.quantize_mx(
+                out=y_codes[:, h, a:b].bitcast(FP8X4), scales=y_plane[:, h, a:b], in_=y_bf[h, a][:]
+            )
+
+        def store_codes(h0, h1, a, b):
+            nc.sync.dma_start(
+                out=words(out_1[h0:h1], "h p n t -> p h (n t)")[:, :, a:b],
+                in_=y_codes[:, h0:h1, a:b],
+            )
+
+        def store_plane(a, b):
+            for q in range(4):
+                nc.sync.dma_start(
+                    out=out_2[:, 4 * q : 4 * q + 4, a:b].rearrange("h r n -> r h n").bitcast(I32),
+                    in_=y_plane[32 * q : 32 * q + 4, :, a:b].bitcast(I32),
+                )
+
+        def stage1_pair(pair, h):
+            stage1(2 * pair, h)
+            stage1(2 * pair + 1, h)
+
+        def residual_pair(pair, h):
+            residual(2 * pair, h)
+            residual(2 * pair + 1, h)
+
+        clear(ls_raw[0])
+        clear(o_plane[0])
+        clear(ls_raw[1])
+        clear(o_plane[1])
+        load_o(0)
+        load_ls(0, 0)
+        load_l(0)
+        for q in range(1, 4):
+            load_ls(0, q)
+        for q in range(4):
+            load_os(0, q)
+        nc.sync.dma_start(out=gain_raw[:], in_=gain.rearrange("(h p t) -> p h t", h=H, t=PACK))
+        load_o(1)
+        load_q(0)
+        load_l(1)
+        for q in range(4):
+            load_ls(1, q)
+        load_u(0, 0)
+        load_q(1)
+        load_u(0, 1)
+        load_o(2)
+        for q in range(4):
+            load_os(1, q)
+        load_c(0, 0)
+        load_u(1, 0)
+        load_c(0, 1)
+        load_u(1, 1)
+        load_c(1, 0)
+        load_o(3)
+        load_c(1, 1)
+        load_u(2, 0)
+        load_c(2, 0)
+        load_u(2, 1)
+        load_c(2, 1)
+
+        order_ls(0)
+        for t in range(PACK):
+            order_l(0, t, t + 1)
+        nc.scalar.activation(out=gain_pos[:], in_=gain_raw[:], func=ACT.Copy)
+        nc.vector.tensor_scalar(out=gain_neg[:], in0=gain_raw[:], scalar1=-1.0, scalar2=None, op0=ALU.mult)
+        stage1_pair(0, 0)
+        group_q(0, 0, nc.scalar.copy)
+        group_q(0, 1, nc.vector.tensor_copy)
+        order_l(1, 0, PACK)
+        order_ls(1)
+        stage1_pair(1, 0)
+        quantize_q(0, 1)
+        stage1_pair(0, 1)
+        quantize_q(0, 0)
+        group_q(1, 0, nc.scalar.copy)
+        residual_pair(0, 0)
+        residual(2, 0)
+        quantize_r(0, 0)
+        residual(3, 0)
+        stage1_pair(1, 1)
+        group_q(1, 1, nc.scalar.copy)
+        residual(0, 1)
+        quantize_r(1, 0)
+        residual(1, 1)
+        quantize_q(1, 0)
+        quantize_r(0, 1)
+        residual_pair(1, 1)
+        stage1_pair(2, 0)
+        scale_c(0, 0, 512)
+        quantize_r(1, 1)
+        quantize_q(1, 1)
+        residual_pair(2, 0)
+        stage2(0, 0, 512)
+        scale_c(1, 0, 512)
+        command(0, 0, 512, 0, 1)
+        quantize_r(2, 0)
+        command(0, 0, 512, 1, 4)
+        store_y(0, 0, 512)
+        stage1_pair(2, 1)
+        round_y(0, 0, 512)
+        residual_pair(2, 1)
+        stage2(1, 0, 512)
+        scale_c(0, 512, 1024)
+        command(1, 0, 512, 0, 1)
+        quantize_r(2, 1)
+        command(1, 0, 512, 1, 4)
+        store_y(1, 0, 512)
+        round_y(1, 0, 512)
+        scale_c(1, 512, 1024)
+        quantize_y(0, 0, 512)
+        pending = (0, 512)
+        for pair in range(3, 6):
+            a, b = (pair - 1) * PAIR, pair * PAIR
+            stage1_pair(pair, 0)
+            residual_pair(pair, 0)
+            stage2(0, a, b)
+            command(0, a, b, 0, 1)
+            quantize_r(pair, 0)
+            command(0, a, b, 1, 4)
+            store_y(0, a, b)
+            quantize_y(1, pending[0], pending[1])
+            store_codes(0, H, pending[0], pending[1])
+            round_y(0, a, b)
+            if pair == 5:
+                break
+            stage1_pair(pair, 1)
+            residual_pair(pair, 1)
+            stage2(1, a, b)
+            command(1, a, b, 0, 1)
+            quantize_r(pair, 1)
+            command(1, a, b, 1, 4)
+            quantize_y(0, a, b)
+            store_y(1, a, b)
+            round_y(1, a, b)
+            scale_c(pair - 3, 1024, 1536)
+            pending = (a, b)
+        store_plane(0, 1024)
+        stage2(1, a, b)
+        command(1, a, b)
+        store_y(1, a, b)
+        round_y(1, a, b)
+        stage1(10, 1)
+        residual(10, 1)
+        quantize_y(0, a, b)
+        quantize_r(5, 1, 0, BLK)
+        stage1(11, 1)
+        residual(11, 1)
+        quantize_y(1, a, b)
+        quantize_r(5, 1, BLK, PAIR)
+        store_codes(0, H, a, b)
+        tail = [(h, x, x + BLK) for x in (1280, 1408) for h in range(H)]
+        for n, (h, x, z) in enumerate(tail):
+            stage2(h, x, z)
+            command(h, x, z)
+            store_y(h, x, z)
+            round_y(h, x, z)
+            if n == 2:
+                quantize_y(*tail[0])
+        quantize_y(*tail[1])
+        store_codes(0, H, 1280, 1408)
+        quantize_y(*tail[2])
+        quantize_y(*tail[3])
+        store_codes(0, H, 1408, B)
+        store_plane(1024, B)

@@ -24,7 +24,7 @@ PAIR = 256
 BANKS = 8
 
 O_CHUNKS = [(0, 256), (256, 512), (512, 1024), (1024, 1536)]
-OS_CHUNKS = [(0, 512), (512, 1536)]
+OS_CHUNKS = [(0, 512), (512, 1024), (1024, 1536)]
 U_CHUNKS = [(0, 512), (512, 1024), (1024, 1536)]
 C_CHUNKS = [(0, 512), (512, 1024), (1024, 1536)]
 
@@ -86,8 +86,8 @@ def tile_disturbance_observer_command_k5_kernel(
 
         def load_plane(plane, scales, a, b, q):
             nc.sync.dma_start(
-                out=plane[32 * q : 32 * q + 4, :, :].bitcast(I32),
-                in_=scales[:, 4 * q : 4 * q + 4, a:b].rearrange("g r n -> r g n").bitcast(I32),
+                out=plane[q:P:32, :, :].bitcast(I32),
+                in_=scales[:, q:16:4, a:b].rearrange("g r n -> r g n").bitcast(I32),
             )
 
         def load_codes(dst, src, a, b):
@@ -235,9 +235,9 @@ def tile_disturbance_observer_command_k5_kernel(
                 in_=y_sb[h][:, :, a:b],
             )
 
-        def round_y(h, a, b):
+        def round_y(h, a, b, copy=nc.scalar.copy):
             y_bf[h, a] = ring.tile([P, (b - a) * PACK], BF16, name="y_bf", tag="y_bf", bufs=4, align_bytes=64)
-            nc.scalar.copy(
+            copy(
                 out=y_bf[h, a][:].rearrange("p (x i t) -> p x t i", i=4, t=PACK),
                 in_=y_sb[h][:, :, a:b].rearrange("p t (x i) -> p x t i", i=4),
             )
@@ -256,8 +256,8 @@ def tile_disturbance_observer_command_k5_kernel(
         def store_plane(a, b):
             for q in range(4):
                 nc.sync.dma_start(
-                    out=out_2[:, 4 * q : 4 * q + 4, a:b].rearrange("h r n -> r h n").bitcast(I32),
-                    in_=y_plane[32 * q : 32 * q + 4, :, a:b].bitcast(I32),
+                    out=out_2[:, q:16:4, a:b].rearrange("h r n -> r h n").bitcast(I32),
+                    in_=y_plane[q:P:32, :, a:b].bitcast(I32),
                 )
 
         def stage1_pair(pair, h):
@@ -272,11 +272,11 @@ def tile_disturbance_observer_command_k5_kernel(
         clear(o_plane[0])
         clear(ls_raw[1])
         clear(o_plane[1])
+        clear(o_plane[2])
         load_o(0)
-        load_ls(0, 0)
-        load_l(0)
-        for q in range(1, 4):
+        for q in range(4):
             load_ls(0, q)
+        load_l(0)
         for q in range(4):
             load_os(0, q)
         nc.sync.dma_start(out=gain_raw[:], in_=gain.rearrange("(h p t) -> p h t", h=H, t=PACK))
@@ -297,6 +297,8 @@ def tile_disturbance_observer_command_k5_kernel(
         load_u(1, 1)
         load_c(1, 0)
         load_o(3)
+        for q in range(4):
+            load_os(2, q)
         load_c(1, 1)
         load_u(2, 0)
         load_c(2, 0)
@@ -354,7 +356,7 @@ def tile_disturbance_observer_command_k5_kernel(
         scale_c(1, 512, 1024)
         quantize_y(0, 0, 512)
         pending = (0, 512)
-        for pair in range(3, 6):
+        for pair in range(3, 5):
             a, b = (pair - 1) * PAIR, pair * PAIR
             stage1_pair(pair, 0)
             residual_pair(pair, 0)
@@ -365,9 +367,11 @@ def tile_disturbance_observer_command_k5_kernel(
             store_y(0, a, b)
             quantize_y(1, pending[0], pending[1])
             store_codes(0, H, pending[0], pending[1])
+            if pair == 4:
+                store_plane(0, 768)
             round_y(0, a, b)
-            if pair == 5:
-                break
+            if pair == 4:
+                scale_c(1, 1024, 1536)
             stage1_pair(pair, 1)
             residual_pair(pair, 1)
             stage2(1, a, b)
@@ -377,33 +381,59 @@ def tile_disturbance_observer_command_k5_kernel(
             quantize_y(0, a, b)
             store_y(1, a, b)
             round_y(1, a, b)
-            scale_c(pair - 3, 1024, 1536)
+            if pair == 3:
+                scale_c(0, 1024, 1536)
             pending = (a, b)
-        store_plane(0, 1024)
-        stage2(1, a, b)
-        command(1, a, b)
-        store_y(1, a, b)
-        round_y(1, a, b)
+        a, b = 1024, 1280
+        stage1(10, 0)
+        residual(10, 0)
+        stage2(0, a, b)
+        command(0, a, b, 0, 1)
+        quantize_r(5, 0, 0, BLK)
+        command(0, a, b, 1, 4)
+        store_y(0, a, b)
+        round_y(0, a, b)
+        quantize_y(1, 768, 1024)
+        store_codes(0, H, 768, 1024)
         stage1(10, 1)
         residual(10, 1)
-        quantize_y(0, a, b)
+        stage2(1, a, b)
+        command(1, a, b, 0, 1)
         quantize_r(5, 1, 0, BLK)
+        command(1, a, b, 1, 4)
+        store_y(1, a, b)
+        round_y(1, a, b)
+        quantize_y(0, a, b)
+        stage1(11, 0)
+        residual(11, 0)
+        stage2(0, 1280, 1408)
+        command(0, 1280, 1408, 0, 1)
+        quantize_r(5, 0, BLK, PAIR)
+        command(0, 1280, 1408, 1, 4)
+        store_y(0, 1280, 1408)
+        round_y(0, 1280, 1408)
+        quantize_y(1, a, b)
+        store_codes(0, H, a, b)
+        store_plane(768, b)
         stage1(11, 1)
         residual(11, 1)
-        quantize_y(1, a, b)
+        quantize_y(0, 1280, 1408)
         quantize_r(5, 1, BLK, PAIR)
-        store_codes(0, H, a, b)
-        tail = [(h, x, x + BLK) for x in (1280, 1408) for h in range(H)]
-        for n, (h, x, z) in enumerate(tail):
-            stage2(h, x, z)
-            command(h, x, z)
-            store_y(h, x, z)
-            round_y(h, x, z)
-            if n == 2:
-                quantize_y(*tail[0])
-        quantize_y(*tail[1])
+        stage2(1, 1280, 1408)
+        command(1, 1280, 1408)
+        store_y(1, 1280, 1408)
+        round_y(1, 1280, 1408)
+        stage2(0, 1408, B)
+        command(0, 1408, B)
+        store_y(0, 1408, B)
+        round_y(0, 1408, B)
+        quantize_y(1, 1280, 1408)
         store_codes(0, H, 1280, 1408)
-        quantize_y(*tail[2])
-        quantize_y(*tail[3])
+        stage2(1, 1408, B)
+        command(1, 1408, B)
+        store_y(1, 1408, B)
+        quantize_y(0, 1408, B)
+        round_y(1, 1408, B, nc.vector.tensor_copy)
+        quantize_y(1, 1408, B)
         store_codes(0, H, 1408, B)
-        store_plane(1024, B)
+        store_plane(1280, B)

@@ -26,6 +26,7 @@ BANKS = 8
 O_CHUNKS = [(0, 256), (256, 512), (512, 1024), (1024, 1536)]
 OS_CHUNKS = [(0, 512), (512, 1024), (1024, 1536)]
 U_CHUNKS = [(0, 512), (512, 1024), (1024, 1536)]
+R_CHUNKS = [(0, 256), (256, 512), (512, 1024), (1024, 1280), (1280, 1408), (1408, 1536)]
 C_CHUNKS = [(0, 512), (512, 1024), (1024, 1536)]
 
 
@@ -54,7 +55,7 @@ def tile_disturbance_observer_command_k5_kernel(
         o_plane = [kept("o_plane%d" % n, [P, G1, b - a], U8) for n, (a, b) in enumerate(OS_CHUNKS)]
         u_sb = [[kept("u%d_%d" % (n, h), [P, PACK, b - a], BF16) for h in range(H)] for n, (a, b) in enumerate(U_CHUNKS)]
         c_sb = [[kept("c%d_%d" % (n, h), [P, PACK, b - a], BF16) for h in range(H)] for n, (a, b) in enumerate(C_CHUNKS)]
-        q_raw = [kept("q_raw%d" % g, [P, PACK, T], BF16) for g in range(H)]
+        q_raw = [[kept("q_raw%d_%d" % (g, h), [P, PACK, PASS], BF16) for h in range(H)] for g in range(H)]
         q_codes = [[kept("q_codes%d_%d" % (g, h), [P, PASS], I32) for h in range(H)] for g in range(H)]
         q_plane = [[kept("q_plane%d_%d" % (g, h), [P, PASS], U8) for h in range(H)] for g in range(H)]
         r_codes = [kept("r_codes%d" % g, [P, B], I32) for g in range(H)]
@@ -123,8 +124,8 @@ def tile_disturbance_observer_command_k5_kernel(
         def load_u(n, h):
             load_r_order(u_sb[n][h], u, h, U_CHUNKS[n][0], U_CHUNKS[n][1])
 
-        def load_q(g):
-            load_r_order(q_raw[g], qf, g, 0, T)
+        def load_q(g, h):
+            load_r_order(q_raw[g][h], qf, g, PASS * h, PASS * (h + 1))
 
         def order_l(h, t0, t1):
             src = words(l_raw[h][:], "p g n -> p (g n)").rearrange("p (x t e) -> p t x e", t=PACK, e=2)
@@ -157,32 +158,32 @@ def tile_disturbance_observer_command_k5_kernel(
                     )
 
         def residual(blk, h):
-            if blk % 2 == 0:
-                r_bf[blk // 2, h] = ring.tile([P, PAIR * PACK], BF16, name="r_bf", tag="r_bf", align_bytes=64)
+            n = find(R_CHUNKS, blk * BLK)
+            a, b = R_CHUNKS[n]
+            if blk * BLK == a:
+                r_bf[n, h] = ring.tile([P, (b - a) * PACK], BF16, name="r_bf", tag="r_bf", align_bytes=64)
             col = blk * BLK
-            n = find(U_CHUNKS, col)
-            uc = col - U_CHUNKS[n][0]
-            half = PASS * (blk % 2)
+            nu = find(U_CHUNKS, col)
+            uc = col - U_CHUNKS[nu][0]
+            at = PACK * (col - a)
             nc.vector.tensor_tensor(
-                out=r_bf[blk // 2, h][:, half : half + PASS].rearrange("p (x i t) -> p x t i", i=4, t=PACK),
+                out=r_bf[n, h][:, at : at + PASS].rearrange("p (x i t) -> p x t i", i=4, t=PACK),
                 in0=s1_bank[blk, h][:].rearrange("p (t x i) -> p x t i", t=PACK, i=4),
-                in1=u_sb[n][h][:, :, uc : uc + BLK].rearrange("p t (x i) -> p x t i", i=4),
+                in1=u_sb[nu][h][:, :, uc : uc + BLK].rearrange("p t (x i) -> p x t i", i=4),
                 op=ALU.subtract,
             )
 
-        def quantize_r(pair, h, lo=0, hi=PAIR):
-            a = pair * PAIR
+        def quantize_r(n, h):
+            a, b = R_CHUNKS[n]
             nc.vector.quantize_mx(
-                out=r_codes[h][:, a + lo : a + hi].bitcast(FP8X4),
-                scales=r_plane[h][:, a + lo : a + hi],
-                in_=r_bf[pair, h][:, PACK * lo : PACK * hi],
+                out=r_codes[h][:, a:b].bitcast(FP8X4), scales=r_plane[h][:, a:b], in_=r_bf[n, h][:]
             )
 
         def group_q(g, h, copy):
             q_bf[g, h] = ring.tile([P, PASS * PACK], BF16, name="q_bf", tag="q_bf", align_bytes=64)
             copy(
                 out=q_bf[g, h][:].rearrange("p (t m j) -> p t m j", t=PACK, j=PACK),
-                in_=q_raw[g][:, :, PASS * h : PASS * (h + 1)].rearrange("p j (m t) -> p t m j", t=PACK),
+                in_=q_raw[g][h][:].rearrange("p j (m t) -> p t m j", t=PACK),
             )
 
         def quantize_q(g, h):
@@ -235,11 +236,14 @@ def tile_disturbance_observer_command_k5_kernel(
                 in_=y_sb[h][:, :, a:b],
             )
 
-        def round_y(h, a, b, copy=nc.scalar.copy):
-            y_bf[h, a] = ring.tile([P, (b - a) * PACK], BF16, name="y_bf", tag="y_bf", bufs=4, align_bytes=64)
+        def round_y(h, a, b, lo=None, hi=None, copy=nc.scalar.copy):
+            lo = a if lo is None else lo
+            hi = b if hi is None else hi
+            if lo == a:
+                y_bf[h, a] = ring.tile([P, (b - a) * PACK], BF16, name="y_bf", tag="y_bf", align_bytes=64)
             copy(
-                out=y_bf[h, a][:].rearrange("p (x i t) -> p x t i", i=4, t=PACK),
-                in_=y_sb[h][:, :, a:b].rearrange("p t (x i) -> p x t i", i=4),
+                out=y_bf[h, a][:, PACK * (lo - a) : PACK * (hi - a)].rearrange("p (x i t) -> p x t i", i=4, t=PACK),
+                in_=y_sb[h][:, :, lo:hi].rearrange("p t (x i) -> p x t i", i=4),
             )
 
         def quantize_y(h, a, b):
@@ -274,166 +278,178 @@ def tile_disturbance_observer_command_k5_kernel(
         clear(o_plane[1])
         clear(o_plane[2])
         load_o(0)
+        nc.sync.dma_start(out=gain_raw[:], in_=gain.rearrange("(h p t) -> p h t", h=H, t=PACK))
         for q in range(4):
             load_ls(0, q)
         load_l(0)
         for q in range(4):
             load_os(0, q)
-        nc.sync.dma_start(out=gain_raw[:], in_=gain.rearrange("(h p t) -> p h t", h=H, t=PACK))
         load_o(1)
-        load_q(0)
-        load_l(1)
+        load_q(0, 0)
         for q in range(4):
             load_ls(1, q)
+        load_l(1)
         load_u(0, 0)
-        load_q(1)
+        load_q(1, 0)
         load_u(0, 1)
-        load_o(2)
         for q in range(4):
             load_os(1, q)
         load_c(0, 0)
+        load_o(2)
+        load_q(0, 1)
+        load_q(1, 1)
         load_u(1, 0)
         load_c(0, 1)
         load_u(1, 1)
         load_c(1, 0)
-        load_o(3)
+        load_c(1, 1)
         for q in range(4):
             load_os(2, q)
-        load_c(1, 1)
+        load_o(3)
         load_u(2, 0)
-        load_c(2, 0)
         load_u(2, 1)
+        load_c(2, 0)
         load_c(2, 1)
-
         order_ls(0)
-        for t in range(PACK):
-            order_l(0, t, t + 1)
+        order_l(0, 0, 2)
+        order_l(0, 2, 4)
         nc.scalar.activation(out=gain_pos[:], in_=gain_raw[:], func=ACT.Copy)
         nc.vector.tensor_scalar(out=gain_neg[:], in0=gain_raw[:], scalar1=-1.0, scalar2=None, op0=ALU.mult)
-        stage1_pair(0, 0)
+        stage1(0, 0)
+        stage1(1, 0)
         group_q(0, 0, nc.scalar.copy)
-        group_q(0, 1, nc.vector.tensor_copy)
-        order_l(1, 0, PACK)
         order_ls(1)
-        stage1_pair(1, 0)
-        quantize_q(0, 1)
-        stage1_pair(0, 1)
+        order_l(1, 0, PACK)
+        stage1(2, 0)
+        stage1(0, 1)
+        stage1(1, 1)
         quantize_q(0, 0)
-        group_q(1, 0, nc.scalar.copy)
-        residual_pair(0, 0)
+        residual(0, 0)
+        residual(1, 0)
         residual(2, 0)
         quantize_r(0, 0)
-        residual(3, 0)
-        stage1_pair(1, 1)
-        group_q(1, 1, nc.scalar.copy)
+        group_q(1, 0, nc.scalar.copy)
         residual(0, 1)
-        quantize_r(1, 0)
         residual(1, 1)
+        stage1(3, 0)
+        stage1(2, 1)
+        stage1(3, 1)
+        residual(3, 0)
         quantize_q(1, 0)
         quantize_r(0, 1)
-        residual_pair(1, 1)
-        stage1_pair(2, 0)
         scale_c(0, 0, 512)
+        residual(2, 1)
+        quantize_r(1, 0)
+        residual(3, 1)
+        stage2(0, 0, 256)
+        group_q(0, 1, nc.scalar.copy)
+        command(0, 0, 256, 0, 1)
         quantize_r(1, 1)
-        quantize_q(1, 1)
-        residual_pair(2, 0)
-        stage2(0, 0, 512)
-        scale_c(1, 0, 512)
-        command(0, 0, 512, 0, 1)
-        quantize_r(2, 0)
-        command(0, 0, 512, 1, 4)
+        command(0, 0, 256, 1, 4)
+        stage1(4, 0)
+        stage2(0, 256, 512)
+        command(0, 256, 512)
         store_y(0, 0, 512)
-        stage1_pair(2, 1)
+        group_q(1, 1, nc.scalar.copy)
+        stage1(5, 0)
+        stage1(4, 1)
+        stage1(5, 1)
+        residual(4, 0)
+        quantize_q(0, 1)
+        residual(5, 0)
+        quantize_q(1, 1)
+        residual(4, 1)
+        residual(5, 1)
+        scale_c(1, 0, 512)
         round_y(0, 0, 512)
-        residual_pair(2, 1)
+        stage1(6, 0)
         stage2(1, 0, 512)
-        scale_c(0, 512, 1024)
-        command(1, 0, 512, 0, 1)
-        quantize_r(2, 1)
-        command(1, 0, 512, 1, 4)
+        command(1, 0, 512)
         store_y(1, 0, 512)
         round_y(1, 0, 512)
+        scale_c(0, 512, 1024)
         scale_c(1, 512, 1024)
+        stage1(7, 0)
+        residual(6, 0)
+        residual(7, 0)
         quantize_y(0, 0, 512)
-        pending = (0, 512)
-        for pair in range(3, 5):
-            a, b = (pair - 1) * PAIR, pair * PAIR
-            stage1_pair(pair, 0)
-            residual_pair(pair, 0)
-            stage2(0, a, b)
-            command(0, a, b, 0, 1)
-            quantize_r(pair, 0)
-            command(0, a, b, 1, 4)
-            store_y(0, a, b)
-            quantize_y(1, pending[0], pending[1])
-            store_codes(0, H, pending[0], pending[1])
-            if pair == 4:
-                store_plane(0, 768)
-            round_y(0, a, b)
-            if pair == 4:
-                scale_c(1, 1024, 1536)
-            stage1_pair(pair, 1)
-            residual_pair(pair, 1)
-            stage2(1, a, b)
-            command(1, a, b, 0, 1)
-            quantize_r(pair, 1)
-            command(1, a, b, 1, 4)
-            quantize_y(0, a, b)
-            store_y(1, a, b)
-            round_y(1, a, b)
-            if pair == 3:
-                scale_c(0, 1024, 1536)
-            pending = (a, b)
-        a, b = 1024, 1280
+        stage1(6, 1)
+        stage1(7, 1)
+        residual(6, 1)
+        quantize_r(2, 0)
+        residual(7, 1)
+        quantize_y(1, 0, 512)
+        quantize_r(2, 1)
+        store_codes(0, 2, 0, 512)
+        stage1(8, 0)
+        stage1(9, 0)
+        residual(8, 0)
+        residual(9, 0)
+        stage2(0, 512, 1024)
+        command(0, 512, 1024)
+        store_y(0, 512, 1024)
+        round_y(0, 512, 1024)
+        scale_c(0, 1024, 1536)
+        quantize_r(3, 0)
+        stage1(8, 1)
+        residual(8, 1)
+        stage2(1, 512, 1024)
+        command(1, 512, 1024)
+        store_y(1, 512, 1024)
+        round_y(1, 512, 1024)
+        scale_c(1, 1024, 1536)
+        stage1(9, 1)
+        residual(9, 1)
+        quantize_r(3, 1)
+        quantize_y(0, 512, 1024)
         stage1(10, 0)
         residual(10, 0)
-        stage2(0, a, b)
-        command(0, a, b, 0, 1)
-        quantize_r(5, 0, 0, BLK)
-        command(0, a, b, 1, 4)
-        store_y(0, a, b)
-        round_y(0, a, b)
-        quantize_y(1, 768, 1024)
-        store_codes(0, H, 768, 1024)
+        stage2(0, 1024, 1280)
+        command(0, 1024, 1280, 0, 1)
+        quantize_r(4, 0)
+        command(0, 1024, 1280, 1, 4)
+        store_y(0, 1024, 1280)
+        round_y(0, 1024, 1280)
         stage1(10, 1)
         residual(10, 1)
-        stage2(1, a, b)
-        command(1, a, b, 0, 1)
-        quantize_r(5, 1, 0, BLK)
-        command(1, a, b, 1, 4)
-        store_y(1, a, b)
-        round_y(1, a, b)
-        quantize_y(0, a, b)
+        quantize_y(1, 512, 1024)
+        store_codes(0, 2, 512, 1024)
+        quantize_r(4, 1)
+        stage2(1, 1024, 1280)
+        command(1, 1024, 1280)
+        store_y(1, 1024, 1280)
+        store_plane(0, 1024)
+        round_y(1, 1024, 1280)
         stage1(11, 0)
         residual(11, 0)
         stage2(0, 1280, 1408)
-        command(0, 1280, 1408, 0, 1)
-        quantize_r(5, 0, BLK, PAIR)
-        command(0, 1280, 1408, 1, 4)
+        command(0, 1280, 1408)
         store_y(0, 1280, 1408)
         round_y(0, 1280, 1408)
-        quantize_y(1, a, b)
-        store_codes(0, H, a, b)
-        store_plane(768, b)
+        quantize_r(5, 0)
         stage1(11, 1)
         residual(11, 1)
-        quantize_y(0, 1280, 1408)
-        quantize_r(5, 1, BLK, PAIR)
+        quantize_y(0, 1024, 1280)
+        quantize_r(5, 1)
+        quantize_y(1, 1024, 1280)
+        store_codes(0, 2, 1024, 1280)
         stage2(1, 1280, 1408)
         command(1, 1280, 1408)
         store_y(1, 1280, 1408)
         round_y(1, 1280, 1408)
-        stage2(0, 1408, B)
-        command(0, 1408, B)
-        store_y(0, 1408, B)
-        round_y(0, 1408, B)
+        quantize_y(0, 1280, 1408)
+        stage2(0, 1408, 1536)
+        command(0, 1408, 1536)
+        store_y(0, 1408, 1536)
+        round_y(0, 1408, 1536)
+        stage2(1, 1408, 1536)
+        command(1, 1408, 1536)
+        store_y(1, 1408, 1536)
+        round_y(1, 1408, 1536, 1408, 1472)
         quantize_y(1, 1280, 1408)
-        store_codes(0, H, 1280, 1408)
-        stage2(1, 1408, B)
-        command(1, 1408, B)
-        store_y(1, 1408, B)
-        quantize_y(0, 1408, B)
-        round_y(1, 1408, B, nc.vector.tensor_copy)
-        quantize_y(1, 1408, B)
-        store_codes(0, H, 1408, B)
-        store_plane(1280, B)
+        store_codes(0, 2, 1280, 1408)
+        round_y(1, 1408, 1536, 1472, 1536, nc.vector.tensor_copy)
+        quantize_y(0, 1408, 1536)
+        quantize_y(1, 1408, 1536)
+        store_codes(0, 2, 1408, 1536)
+        store_plane(1024, 1536)

from contextlib import ExitStack

import concourse.mybir as mybir

K, T, B = 2048, 1024, 1536
FLOPS = 2 * K * T * B + 2 * T * T * B

F32 = mybir.dt.float32
BF16 = mybir.dt.bfloat16
I32 = mybir.dt.int32
U8 = mybir.dt.uint8
FP8X4 = mybir.dt.float8_e4m3fn_x4
FP4X4 = mybir.dt.float4_e2m1fn_x4
ALU = mybir.AluOpType
ACT = mybir.ActivationFunctionType

P = 128
PACK = 4
PASS = P * PACK
G1 = K // PASS
H = T // PASS
BLK = 128
PAIR = 256
BANKS = 8

O_CHUNKS = [(0, 256), (256, 512), (512, 1024), (1024, 1536)]
OS_CHUNKS = [(0, 512), (512, 1024), (1024, 1536)]
U_CHUNKS = [(0, 512), (512, 1024), (1024, 1536)]
R_CHUNKS = [(0, 256), (256, 512), (512, 1024), (1024, 1280), (1280, 1408), (1408, 1536)]
C_CHUNKS = [(0, 512), (512, 1024), (1024, 1536)]


def find(chunks, col):
    return [n for n, (a, b) in enumerate(chunks) if a <= col < b][0]


def tile_disturbance_observer_command_k5_kernel(
    tc, l_words, l_scales, o_words, o_scales, u, qf, c, gain, out_0, out_1, out_2
):
    nc = tc.nc
    with ExitStack() as ctx:
        keep = ctx.enter_context(tc.tile_pool(name="keep", bufs=1))
        ring = ctx.enter_context(tc.tile_pool(name="ring", bufs=3))
        psum = ctx.enter_context(tc.psum_pool(name="psum", bufs=1))
        ctx.enter_context(tc.manual_schedule())

        def kept(name, shape, dtype):
            return keep.tile(shape, dtype, name=name, align_bytes=64)

        l_raw = [kept("l_raw%d" % h, [P, G1, 2 * PASS], U8) for h in range(H)]
        ls_raw = [kept("ls_raw%d" % h, [P, G1, PASS], U8) for h in range(H)]
        l_codes = [kept("l_codes%d" % h, [P, PACK, G1, 2 * P], U8) for h in range(H)]
        l_plane = [kept("l_plane%d" % h, [P, PACK, G1, P], U8) for h in range(H)]
        o_codes = [kept("o_codes%d" % n, [P, G1, 2 * (b - a)], U8) for n, (a, b) in enumerate(O_CHUNKS)]
        o_plane = [kept("o_plane%d" % n, [P, G1, b - a], U8) for n, (a, b) in enumerate(OS_CHUNKS)]
        u_sb = [[kept("u%d_%d" % (n, h), [P, PACK, b - a], BF16) for h in range(H)] for n, (a, b) in enumerate(U_CHUNKS)]
        c_sb = [[kept("c%d_%d" % (n, h), [P, PACK, b - a], BF16) for h in range(H)] for n, (a, b) in enumerate(C_CHUNKS)]
        q_raw = [[kept("q_raw%d_%d" % (g, h), [P, PACK, PASS], BF16) for h in range(H)] for g in range(H)]
        q_codes = [[kept("q_codes%d_%d" % (g, h), [P, PASS], I32) for h in range(H)] for g in range(H)]
        q_plane = [[kept("q_plane%d_%d" % (g, h), [P, PASS], U8) for h in range(H)] for g in range(H)]
        r_codes = [kept("r_codes%d" % g, [P, B], I32) for g in range(H)]
        r_plane = [kept("r_plane%d" % g, [P, B], U8) for g in range(H)]
        y_sb = [kept("y%d" % h, [P, PACK, B], F32) for h in range(H)]
        y_codes = kept("y_codes", [P, H, B], I32)
        y_plane = kept("y_plane", [P, H, B], U8)
        gain_raw = kept("gain_raw", [P, H, PACK], BF16)
        gain_pos = kept("gain_pos", [P, H, PACK], F32)
        gain_neg = kept("gain_neg", [P, H, PACK], F32)

        used_banks = []
        s1_bank = {}
        s2_bank = {}
        r_bf = {}
        y_bf = {}
        q_bf = {}

        def new_bank():
            n = len(used_banks) % BANKS
            used_banks.append(n)
            return psum.tile([P, PASS], F32, name="bank%d" % n, tag="bank%d" % n)

        def words(ap, pattern):
            return ap.rearrange(pattern).bitcast(I32)

        def clear(plane):
            nc.vector.memset(words(plane[:], "p g n -> p (g n)"), 0)

        def load_plane(plane, scales, a, b, q):
            nc.sync.dma_start(
                out=plane[q:P:32, :, :].bitcast(I32),
                in_=scales[:, q:16:4, a:b].rearrange("g r n -> r g n").bitcast(I32),
            )

        def load_codes(dst, src, a, b):
            nc.sync.dma_start(
                out=dst[:].bitcast(I32),
                in_=src[:, :, 2 * a : 2 * b].rearrange("g p n -> p g n").bitcast(I32),
            )

        def load_r_order(dst, src, g, a, b):
            rows = src[PASS * g : PASS * (g + 1), a:b].rearrange("(c t e) n -> e c t n", t=PACK, e=4)
            for e in range(4):
                nc.sync.dma_start(out=dst[e:P:4, :, :], in_=rows[e])

        def load_c(n, h):
            a, b = C_CHUNKS[n]
            nc.sync.dma_start(
                out=c_sb[n][h][:],
                in_=c[PASS * h : PASS * (h + 1), a:b].rearrange("(p t) n -> p t n", t=PACK),
            )

        def load_ls(h, q):
            load_plane(ls_raw[h], l_scales, PASS * h, PASS * (h + 1), q)

        def load_os(n, q):
            load_plane(o_plane[n], o_scales, OS_CHUNKS[n][0], OS_CHUNKS[n][1], q)

        def load_l(h):
            load_codes(l_raw[h], l_words, PASS * h, PASS * (h + 1))

        def load_o(n):
            load_codes(o_codes[n], o_words, O_CHUNKS[n][0], O_CHUNKS[n][1])

        def load_u(n, h):
            load_r_order(u_sb[n][h], u, h, U_CHUNKS[n][0], U_CHUNKS[n][1])

        def load_q(g, h):
            load_r_order(q_raw[g][h], qf, g, PASS * h, PASS * (h + 1))

        def order_l(h, t0, t1):
            src = words(l_raw[h][:], "p g n -> p (g n)").rearrange("p (x t e) -> p t x e", t=PACK, e=2)
            dst = words(l_codes[h][:], "p t g n -> p (t g n)").rearrange("p (t x e) -> p t x e", t=PACK, e=2)
            nc.vector.tensor_copy(out=dst[:, t0:t1], in_=src[:, t0:t1])

        def order_ls(h):
            src = words(ls_raw[h][:], "p g n -> p (g n)").rearrange("p (x t) -> p t x", t=PACK)
            dst = words(l_plane[h][:], "p t g n -> p (t g n)").rearrange("p (t x) -> p t x", t=PACK)
            nc.vector.tensor_copy(out=dst, in_=src)

        def stage1(blk, h):
            bank = new_bank()
            s1_bank[blk, h] = bank
            col = blk * BLK
            n = find(O_CHUNKS, col)
            ns = find(OS_CHUNKS, col)
            oc = col - O_CHUNKS[n][0]
            sc = col - OS_CHUNKS[ns][0]
            for t in range(PACK):
                for g in range(G1):
                    nc.tensor.matmul_mx(
                        out=bank[:, BLK * t : BLK * (t + 1)],
                        lhsT=l_codes[h][:, t, g, :].bitcast(FP4X4),
                        lhsT_scale=l_plane[h][:, t, g, :],
                        rhs=o_codes[n][:, g, 2 * oc : 2 * (oc + BLK)].bitcast(FP4X4),
                        rhs_scale=o_plane[ns][:, g, sc : sc + BLK],
                        start=(g == 0),
                        stop=(g == G1 - 1),
                    )

        def residual(blk, h):
            n = find(R_CHUNKS, blk * BLK)
            a, b = R_CHUNKS[n]
            if blk * BLK == a:
                r_bf[n, h] = ring.tile([P, (b - a) * PACK], BF16, name="r_bf", tag="r_bf", align_bytes=64)
            col = blk * BLK
            nu = find(U_CHUNKS, col)
            uc = col - U_CHUNKS[nu][0]
            at = PACK * (col - a)
            nc.vector.tensor_tensor(
                out=r_bf[n, h][:, at : at + PASS].rearrange("p (x i t) -> p x t i", i=4, t=PACK),
                in0=s1_bank[blk, h][:].rearrange("p (t x i) -> p x t i", t=PACK, i=4),
                in1=u_sb[nu][h][:, :, uc : uc + BLK].rearrange("p t (x i) -> p x t i", i=4),
                op=ALU.subtract,
            )

        def quantize_r(n, h):
            a, b = R_CHUNKS[n]
            nc.vector.quantize_mx(
                out=r_codes[h][:, a:b].bitcast(FP8X4), scales=r_plane[h][:, a:b], in_=r_bf[n, h][:]
            )

        def group_q(g, h, copy):
            q_bf[g, h] = ring.tile([P, PASS * PACK], BF16, name="q_bf", tag="q_bf", align_bytes=64)
            copy(
                out=q_bf[g, h][:].rearrange("p (t m j) -> p t m j", t=PACK, j=PACK),
                in_=q_raw[g][h][:].rearrange("p j (m t) -> p t m j", t=PACK),
            )

        def quantize_q(g, h):
            nc.vector.quantize_mx(out=q_codes[g][h][:].bitcast(FP8X4), scales=q_plane[g][h][:], in_=q_bf[g, h][:])

        def scale_c(h, a, b):
            n = find(C_CHUNKS, a)
            c0 = C_CHUNKS[n][0]
            for t in range(PACK):
                nc.scalar.activation(
                    out=y_sb[h][:, t, a:b],
                    in_=c_sb[n][h][:, t, a - c0 : b - c0],
                    func=ACT.Copy,
                    scale=gain_pos[:, h, t : t + 1],
                )

        def stage2(h, a, b):
            w = b - a
            per_bank = PASS // w
            for t in range(PACK):
                if t % per_bank == 0:
                    bank = new_bank()
                dst = bank[:, w * (t % per_bank) : w * (t % per_bank + 1)]
                s2_bank[h, a, t] = dst
                for g in range(H):
                    nc.tensor.matmul_mx(
                        out=dst,
                        lhsT=q_codes[g][h][:, P * t : P * (t + 1)].bitcast(FP8X4),
                        lhsT_scale=q_plane[g][h][:, P * t : P * (t + 1)],
                        rhs=r_codes[g][:, a:b].bitcast(FP8X4),
                        rhs_scale=r_plane[g][:, a:b],
                        start=(g == 0),
                        stop=(g == H - 1),
                    )

        def command(h, a, b, t0=0, t1=PACK):
            for t in range(t0, t1):
                nc.vector.scalar_tensor_tensor(
                    out=y_sb[h][:, t, a:b],
                    in0=s2_bank[h, a, t],
                    scalar=gain_neg[:, h, t : t + 1],
                    in1=y_sb[h][:, t, a:b],
                    op0=ALU.mult,
                    op1=ALU.add,
                )

        def store_y(h, a, b):
            nc.sync.dma_start(
                out=out_0[PASS * h : PASS * (h + 1), a:b].rearrange("(p t) n -> p t n", t=PACK),
                in_=y_sb[h][:, :, a:b],
            )

        def round_y(h, a, b, lo=None, hi=None, copy=nc.scalar.copy):
            lo = a if lo is None else lo
            hi = b if hi is None else hi
            if lo == a:
                y_bf[h, a] = ring.tile([P, (b - a) * PACK], BF16, name="y_bf", tag="y_bf", align_bytes=64)
            copy(
                out=y_bf[h, a][:, PACK * (lo - a) : PACK * (hi - a)].rearrange("p (x i t) -> p x t i", i=4, t=PACK),
                in_=y_sb[h][:, :, lo:hi].rearrange("p t (x i) -> p x t i", i=4),
            )

        def quantize_y(h, a, b):
            nc.vector.quantize_mx(
                out=y_codes[:, h, a:b].bitcast(FP8X4), scales=y_plane[:, h, a:b], in_=y_bf[h, a][:]
            )

        def store_codes(h0, h1, a, b):
            nc.sync.dma_start(
                out=words(out_1[h0:h1], "h p n t -> p h (n t)")[:, :, a:b],
                in_=y_codes[:, h0:h1, a:b],
            )

        def store_plane(a, b):
            for q in range(4):
                nc.sync.dma_start(
                    out=out_2[:, q:16:4, a:b].rearrange("h r n -> r h n").bitcast(I32),
                    in_=y_plane[q:P:32, :, a:b].bitcast(I32),
                )

        def stage1_pair(pair, h):
            stage1(2 * pair, h)
            stage1(2 * pair + 1, h)

        def residual_pair(pair, h):
            residual(2 * pair, h)
            residual(2 * pair + 1, h)

        clear(ls_raw[0])
        clear(o_plane[0])
        clear(ls_raw[1])
        clear(o_plane[1])
        clear(o_plane[2])
        load_o(0)
        nc.sync.dma_start(out=gain_raw[:], in_=gain.rearrange("(h p t) -> p h t", h=H, t=PACK))
        for q in range(4):
            load_ls(0, q)
        load_l(0)
        for q in range(4):
            load_os(0, q)
        load_o(1)
        load_q(0, 0)
        for q in range(4):
            load_ls(1, q)
        load_l(1)
        load_u(0, 0)
        load_q(1, 0)
        load_u(0, 1)
        for q in range(4):
            load_os(1, q)
        load_c(0, 0)
        load_o(2)
        load_q(0, 1)
        load_q(1, 1)
        load_u(1, 0)
        load_c(0, 1)
        load_u(1, 1)
        load_c(1, 0)
        load_c(1, 1)
        for q in range(4):
            load_os(2, q)
        load_o(3)
        load_u(2, 0)
        load_u(2, 1)
        load_c(2, 0)
        load_c(2, 1)
        order_ls(0)
        order_l(0, 0, 2)
        order_l(0, 2, 4)
        nc.scalar.activation(out=gain_pos[:], in_=gain_raw[:], func=ACT.Copy)
        nc.vector.tensor_scalar(out=gain_neg[:], in0=gain_raw[:], scalar1=-1.0, scalar2=None, op0=ALU.mult)
        stage1(0, 0)
        stage1(1, 0)
        group_q(0, 0, nc.scalar.copy)
        order_ls(1)
        order_l(1, 0, PACK)
        stage1(2, 0)
        stage1(0, 1)
        stage1(1, 1)
        quantize_q(0, 0)
        residual(0, 0)
        residual(1, 0)
        residual(2, 0)
        quantize_r(0, 0)
        group_q(1, 0, nc.scalar.copy)
        residual(0, 1)
        residual(1, 1)
        stage1(3, 0)
        stage1(2, 1)
        stage1(3, 1)
        residual(3, 0)
        quantize_q(1, 0)
        quantize_r(0, 1)
        scale_c(0, 0, 512)
        residual(2, 1)
        quantize_r(1, 0)
        residual(3, 1)
        stage2(0, 0, 256)
        group_q(0, 1, nc.scalar.copy)
        command(0, 0, 256, 0, 1)
        quantize_r(1, 1)
        command(0, 0, 256, 1, 4)
        stage1(4, 0)
        stage2(0, 256, 512)
        command(0, 256, 512)
        store_y(0, 0, 512)
        group_q(1, 1, nc.scalar.copy)
        stage1(5, 0)
        stage1(4, 1)
        stage1(5, 1)
        residual(4, 0)
        quantize_q(0, 1)
        residual(5, 0)
        quantize_q(1, 1)
        residual(4, 1)
        residual(5, 1)
        scale_c(1, 0, 512)
        round_y(0, 0, 512)
        stage1(6, 0)
        stage2(1, 0, 512)
        command(1, 0, 512)
        store_y(1, 0, 512)
        round_y(1, 0, 512)
        scale_c(0, 512, 1024)
        scale_c(1, 512, 1024)
        stage1(7, 0)
        residual(6, 0)
        residual(7, 0)
        quantize_y(0, 0, 512)
        stage1(6, 1)
        stage1(7, 1)
        residual(6, 1)
        quantize_r(2, 0)
        residual(7, 1)
        quantize_y(1, 0, 512)
        quantize_r(2, 1)
        store_codes(0, 2, 0, 512)
        stage1(8, 0)
        stage1(9, 0)
        residual(8, 0)
        residual(9, 0)
        stage2(0, 512, 1024)
        command(0, 512, 1024)
        store_y(0, 512, 1024)
        round_y(0, 512, 1024)
        scale_c(0, 1024, 1536)
        quantize_r(3, 0)
        stage1(8, 1)
        residual(8, 1)
        stage2(1, 512, 1024)
        command(1, 512, 1024)
        store_y(1, 512, 1024)
        round_y(1, 512, 1024)
        scale_c(1, 1024, 1536)
        stage1(9, 1)
        residual(9, 1)
        quantize_r(3, 1)
        quantize_y(0, 512, 1024)
        stage1(10, 0)
        residual(10, 0)
        stage2(0, 1024, 1280)
        command(0, 1024, 1280, 0, 1)
        quantize_r(4, 0)
        command(0, 1024, 1280, 1, 4)
        store_y(0, 1024, 1280)
        round_y(0, 1024, 1280)
        stage1(10, 1)
        residual(10, 1)
        quantize_y(1, 512, 1024)
        store_codes(0, 2, 512, 1024)
        quantize_r(4, 1)
        stage2(1, 1024, 1280)
        command(1, 1024, 1280)
        store_y(1, 1024, 1280)
        store_plane(0, 1024)
        round_y(1, 1024, 1280)
        stage1(11, 0)
        residual(11, 0)
        stage2(0, 1280, 1408)
        command(0, 1280, 1408)
        store_y(0, 1280, 1408)
        round_y(0, 1280, 1408)
        quantize_r(5, 0)
        stage1(11, 1)
        residual(11, 1)
        quantize_y(0, 1024, 1280)
        quantize_r(5, 1)
        quantize_y(1, 1024, 1280)
        store_codes(0, 2, 1024, 1280)
        stage2(1, 1280, 1408)
        command(1, 1280, 1408)
        store_y(1, 1280, 1408)
        round_y(1, 1280, 1408)
        quantize_y(0, 1280, 1408)
        stage2(0, 1408, 1536)
        command(0, 1408, 1536)
        store_y(0, 1408, 1536)
        round_y(0, 1408, 1536)
        stage2(1, 1408, 1536)
        command(1, 1408, 1536)
        store_y(1, 1408, 1536)
        round_y(1, 1408, 1536, 1408, 1472)
        quantize_y(1, 1280, 1408)
        store_codes(0, 2, 1280, 1408)
        round_y(1, 1408, 1536, 1472, 1536, nc.vector.tensor_copy)
        quantize_y(0, 1408, 1536)
        quantize_y(1, 1408, 1536)
        store_codes(0, 2, 1408, 1536)
        store_plane(1024, 1536)
